import numpy as np
CORES = [24,25,26,27,28,29,30,31,0,8,16]
N = 11
ROOT = 1
WIDTHS = [12,0,64,128,64,64,12,0,12,0,12]
OFF = [0,12,12,76,204,268,332,344,344,356,356]
C = 368
def setup_inputs(rng):
    return {"x": rng.standard_normal((N, 128, C), dtype=np.float32)}
def reference(x):
    YW = max(WIDTHS)
    y = np.full((N, 128, YW), np.nan, x.dtype)
    for r in range(N):
        y[r][:, :WIDTHS[r]] = x[ROOT][:, OFF[r]:OFF[r] + WIDTHS[r]]
    return {"y": y}

@@ -1,0 +1,81 @@
+from concourse.bass import DstId, RemoteDMATransfer
+
+SCRATCH = {
+    "tail": ("dram", [128, 36], "float32"),
+    "b1": ("dram", [128, 76], "float32"),
+    "b2": ("dram", [128, 128], "float32"),
+    "b3": ("dram", [128, 128], "float32"),
+}
+SEMAPHORES = ["ld_t", "ld_23", "ld_1", "sent", "tarr", "arr", "fsent", "stored"]
+
+ROOT = 25
+RELAY = {26: 0, 30: 16}
+TAIL0 = 332
+MAIN = {
+    27: ("b2", 76, 0x00FF),
+    28: ("b3", 204, 0x0F00),
+    29: ("b3", 204, 0xF000),
+    24: ("b1", 0, 0x000F),
+    26: ("b1", 0, 0x00F0),
+}
+
+
+def _bits(m):
+    return bin(m).count("1")
+
+
+def rank_program(g, core, T, topo):
+    rank = T.rank_of(core)
+    if rank is None:
+        return
+    S = T.sem
+    W = T.tables["WIDTHS"]
+    OFF = T.tables["OFF"]
+
+    def xfer(buf, dst, mask, sem):
+        rid, pid, _se = topo.addr(dst)
+        return RemoteDMATransfer(dst_ids=[DstId(rid=rid, pnc=pid)], dma_engine_mask=mask, remote_sem=sem,
+                                 src=T[buf][:], dst=T[buf][:])
+
+    if core == ROOT:
+        sy, sc = g.sync, g.scalar
+        sy.dma_start(T.tail[0:64, :], T.x[0:64, TAIL0:TAIL0 + 36]).then_inc(S.ld_t, 16)
+        sc.dma_start(T.tail[64:128, :], T.x[64:128, TAIL0:TAIL0 + 36]).then_inc(S.ld_t, 16)
+        sy.dma_start(T.b2[:], T.x[:, 76:204]).then_inc(S.ld_23, 16)
+        sc.dma_start(T.b3[:], T.x[:, 204:332]).then_inc(S.ld_23, 16)
+        sy.dma_start(T.b1[:], T.x[:, 0:76]).then_inc(S.ld_1, 16)
+        g.wait_ge(S.ld_t, 32)
+        g.remote_dma_fused([xfer("tail", 26, 0x00FF, S.tarr), xfer("tail", 30, 0xFF00, S.tarr)], local_sem=S.sent)
+        g.wait_ge(S.ld_23, 32)
+        g.remote_dma_fused([xfer(MAIN[c][0], c, MAIN[c][2], S.arr) for c in (27, 28, 29)], local_sem=S.sent)
+        g.wait_ge(S.ld_1, 16)
+        g.remote_dma_fused([xfer(MAIN[c][0], c, MAIN[c][2], S.arr) for c in (24, 26)], local_sem=S.sent)
+        g.wait_ge(S.sent, 16 + 16 + 8)
+        return
+
+    w = W[rank]
+    if core in RELAY:
+        far = RELAY[core]
+        rid, pid, _se = topo.addr(far)
+        g.wait_ge(S.tarr, 8)
+        g.remote_dma(T.tail[:], T.tail[:], S.tarr, S.fsent, pid, rid, 0x00FF)
+
+    if core in MAIN:
+        buf, c0, mask = MAIN[core]
+        o = OFF[rank] - c0
+        g.sync.wait_ge(S.arr, _bits(mask))
+        if o == 0 and T[buf].shape[1] == T.y.shape[1]:
+            g.sync.dma_start(T.y[:], T[buf][:]).then_inc(S.stored, 16)
+        else:
+            g.sync.dma_start(T.y[:, 0:w], T[buf][:, o:o + w]).then_inc(S.stored, 16)
+    elif w > 0:
+        o = OFF[rank] - TAIL0
+        g.sync.wait_ge(S.tarr, 8)
+        if core in RELAY:
+            g.sync.wait_ge(S.fsent, 8)
+        g.sync.dma_start(T.y[:, 0:w], T.tail[:, o:o + w]).then_inc(S.stored, 16)
+
+    if core in RELAY:
+        g.wait_ge(S.fsent, 8)
+    if w > 0:
+        g.wait_ge(S.stored, 16)

@@ -1,23 +1,16 @@
 from concourse.bass import DstId, RemoteDMATransfer
 
-SCRATCH = {
-    "tail": ("dram", [128, 36], "float32"),
-    "b1": ("dram", [128, 76], "float32"),
-    "b2": ("dram", [128, 128], "float32"),
-    "b3": ("dram", [128, 128], "float32"),
-}
-SEMAPHORES = ["ld_t", "ld_23", "ld_1", "sent", "tarr", "arr", "fsent", "stored"]
-
+BLOCKS = {"t8": (344, 356), "t10": (356, 368), "b1": (0, 76), "b2": (76, 204), "b3": (204, 332), "b4": (268, 344)}
+SCRATCH = {k: ("dram", [128, v[1] - v[0]], "float32") for k, v in BLOCKS.items()}
+SEMAPHORES = ["l0", "l1", "l2", "l3", "sent", "tarr", "arr", "fsent", "stored"]
 ROOT = 25
-RELAY = {26: 0, 30: 16}
-TAIL0 = 332
-MAIN = {
-    27: ("b2", 76, 0x00FF),
-    28: ("b3", 204, 0x0F00),
-    29: ("b3", 204, 0xF000),
-    24: ("b1", 0, 0x000F),
-    26: ("b1", 0, 0x00F0),
-}
+LOADS = [("sy", "t8", 0, 128, "l0"), ("sc", "t10", 0, 128, "l0"),
+         ("sy", "b2", 0, 128, "l1"), ("sc", "b3", 0, 128, "l1"),
+         ("sy", "b1", 0, 128, "l2"), ("sc", "b4", 0, 128, "l2")]
+CALLS = [("l0", 32, [("t8", 26, 0x00FF), ("t10", 31, 0xFF00)]),
+         ("l1", 32, [("b2", 27, 0x00FF), ("b3", 28, 0xFF00)]),
+         ("l2", 32, [("b1", 24, 0x000F), ("b1", 26, 0x00F0), ("b4", 29, 0x0F00), ("b4", 30, 0xF000)])]
+FWD = {26: (0, "t8"), 31: (16, "t10")}
 
 
 def _bits(m):
@@ -25,57 +18,51 @@ def _bits(m):
 
 
 def rank_program(g, core, T, topo):
-    rank = T.rank_of(core)
-    if rank is None:
-        return
     S = T.sem
-    W = T.tables["WIDTHS"]
-    OFF = T.tables["OFF"]
+    q = {"sy": g.sync, "sc": g.scalar}
 
-    def xfer(buf, dst, mask, sem):
-        rid, pid, _se = topo.addr(dst)
-        return RemoteDMATransfer(dst_ids=[DstId(rid=rid, pnc=pid)], dma_engine_mask=mask, remote_sem=sem,
-                                 src=T[buf][:], dst=T[buf][:])
+    def sem_of(b):
+        return S.tarr if b[0] == "t" else S.arr
 
     if core == ROOT:
-        sy, sc = g.sync, g.scalar
-        sy.dma_start(T.tail[0:64, :], T.x[0:64, TAIL0:TAIL0 + 36]).then_inc(S.ld_t, 16)
-        sc.dma_start(T.tail[64:128, :], T.x[64:128, TAIL0:TAIL0 + 36]).then_inc(S.ld_t, 16)
-        sy.dma_start(T.b2[:], T.x[:, 76:204]).then_inc(S.ld_23, 16)
-        sc.dma_start(T.b3[:], T.x[:, 204:332]).then_inc(S.ld_23, 16)
-        sy.dma_start(T.b1[:], T.x[:, 0:76]).then_inc(S.ld_1, 16)
-        g.wait_ge(S.ld_t, 32)
-        g.remote_dma_fused([xfer("tail", 26, 0x00FF, S.tarr), xfer("tail", 30, 0xFF00, S.tarr)], local_sem=S.sent)
-        g.wait_ge(S.ld_23, 32)
-        g.remote_dma_fused([xfer(MAIN[c][0], c, MAIN[c][2], S.arr) for c in (27, 28, 29)], local_sem=S.sent)
-        g.wait_ge(S.ld_1, 16)
-        g.remote_dma_fused([xfer(MAIN[c][0], c, MAIN[c][2], S.arr) for c in (24, 26)], local_sem=S.sent)
-        g.wait_ge(S.sent, 16 + 16 + 8)
+        for qn, b, r0, r1, sem in LOADS:
+            c0, c1 = BLOCKS[b]
+            q[qn].dma_start(T[b][r0:r1, :], T.x[r0:r1, c0:c1]).then_inc(S[sem], 16)
+        total = 0
+        for sem, n, trs in CALLS:
+            g.wait_ge(S[sem], n)
+            lst = []
+            for b, dst, mask in trs:
+                rid, pid, _se = topo.addr(dst)
+                lst.append(RemoteDMATransfer(dst_ids=[DstId(rid=rid, pnc=pid)], dma_engine_mask=mask,
+                                             remote_sem=sem_of(b), src=T[b][:], dst=T[b][:]))
+                total += _bits(mask)
+            g.remote_dma_fused(lst, local_sem=S.sent)
+        g.wait_ge(S.sent, total)
         return
 
-    w = W[rank]
-    if core in RELAY:
-        far = RELAY[core]
+    if core in FWD:
+        far, fb = FWD[core]
         rid, pid, _se = topo.addr(far)
         g.wait_ge(S.tarr, 8)
-        g.remote_dma(T.tail[:], T.tail[:], S.tarr, S.fsent, pid, rid, 0x00FF)
+        g.remote_dma(T[fb][:], T[fb][:], S.tarr, S.fsent, pid, rid, 0x00FF)
 
-    if core in MAIN:
-        buf, c0, mask = MAIN[core]
-        o = OFF[rank] - c0
-        g.sync.wait_ge(S.arr, _bits(mask))
-        if o == 0 and T[buf].shape[1] == T.y.shape[1]:
-            g.sync.dma_start(T.y[:], T[buf][:]).then_inc(S.stored, 16)
-        else:
-            g.sync.dma_start(T.y[:, 0:w], T[buf][:, o:o + w]).then_inc(S.stored, 16)
-    elif w > 0:
-        o = OFF[rank] - TAIL0
-        g.sync.wait_ge(S.tarr, 8)
-        if core in RELAY:
+    rank = T.rank_of(core)
+    w = 0 if rank is None else T.tables["WIDTHS"][rank]
+    if w > 0:
+        off = T.tables["OFF"][rank]
+        inc = [(t[0], _bits(t[2])) for c in CALLS for t in c[2] if t[1] == core]
+        inc += [(v[1], 8) for v in FWD.values() if v[0] == core]
+        b, n = [i for i in inc if BLOCKS[i[0]][0] <= off and off + w <= BLOCKS[i[0]][1]][0]
+        g.sync.wait_ge(sem_of(b), n)
+        if core in FWD and FWD[core][1] == b:
             g.sync.wait_ge(S.fsent, 8)
-        g.sync.dma_start(T.y[:, 0:w], T.tail[:, o:o + w]).then_inc(S.stored, 16)
-
-    if core in RELAY:
+        o = off - BLOCKS[b][0]
+        if o == 0 and T[b].shape[1] == T.y.shape[1]:
+            g.sync.dma_start(T.y[:], T[b][:]).then_inc(S.stored, 16)
+        else:
+            g.sync.dma_start(T.y[:, 0:w], T[b][:, o:o + w]).then_inc(S.stored, 16)
+    if core in FWD:
         g.wait_ge(S.fsent, 8)
     if w > 0:
         g.wait_ge(S.stored, 16)

from concourse.bass import DstId, RemoteDMATransfer

BLOCKS = {"t8": (344, 356), "t10": (356, 368), "b1": (0, 76), "b2": (76, 204), "b3": (204, 332), "b4": (268, 344)}
SCRATCH = {k: ("dram", [128, v[1] - v[0]], "float32") for k, v in BLOCKS.items()}
SEMAPHORES = ["l0", "l1", "l2", "l3", "sent", "tarr", "arr", "fsent", "stored"]
ROOT = 25
LOADS = [("sy", "t8", 0, 128, "l0"), ("sc", "t10", 0, 128, "l0"),
         ("sy", "b2", 0, 128, "l1"), ("sc", "b3", 0, 128, "l1"),
         ("sy", "b1", 0, 128, "l2"), ("sc", "b4", 0, 128, "l2")]
CALLS = [("l0", 32, [("t8", 26, 0x00FF), ("t10", 31, 0xFF00)]),
         ("l1", 32, [("b2", 27, 0x00FF), ("b3", 28, 0xFF00)]),
         ("l2", 32, [("b1", 24, 0x000F), ("b1", 26, 0x00F0), ("b4", 29, 0x0F00), ("b4", 30, 0xF000)])]
FWD = {26: (0, "t8"), 31: (16, "t10")}


def _bits(m):
    return bin(m).count("1")


def rank_program(g, core, T, topo):
    S = T.sem
    q = {"sy": g.sync, "sc": g.scalar}

    def sem_of(b):
        return S.tarr if b[0] == "t" else S.arr

    if core == ROOT:
        for qn, b, r0, r1, sem in LOADS:
            c0, c1 = BLOCKS[b]
            q[qn].dma_start(T[b][r0:r1, :], T.x[r0:r1, c0:c1]).then_inc(S[sem], 16)
        total = 0
        for sem, n, trs in CALLS:
            g.wait_ge(S[sem], n)
            lst = []
            for b, dst, mask in trs:
                rid, pid, _se = topo.addr(dst)
                lst.append(RemoteDMATransfer(dst_ids=[DstId(rid=rid, pnc=pid)], dma_engine_mask=mask,
                                             remote_sem=sem_of(b), src=T[b][:], dst=T[b][:]))
                total += _bits(mask)
            g.remote_dma_fused(lst, local_sem=S.sent)
        g.wait_ge(S.sent, total)
        return

    if core in FWD:
        far, fb = FWD[core]
        rid, pid, _se = topo.addr(far)
        g.wait_ge(S.tarr, 8)
        g.remote_dma(T[fb][:], T[fb][:], S.tarr, S.fsent, pid, rid, 0x00FF)

    rank = T.rank_of(core)
    w = 0 if rank is None else T.tables["WIDTHS"][rank]
    if w > 0:
        off = T.tables["OFF"][rank]
        inc = [(t[0], _bits(t[2])) for c in CALLS for t in c[2] if t[1] == core]
        inc += [(v[1], 8) for v in FWD.values() if v[0] == core]
        b, n = [i for i in inc if BLOCKS[i[0]][0] <= off and off + w <= BLOCKS[i[0]][1]][0]
        g.sync.wait_ge(sem_of(b), n)
        if core in FWD and FWD[core][1] == b:
            g.sync.wait_ge(S.fsent, 8)
        o = off - BLOCKS[b][0]
        if o == 0 and T[b].shape[1] == T.y.shape[1]:
            g.sync.dma_start(T.y[:], T[b][:]).then_inc(S.stored, 16)
        else:
            g.sync.dma_start(T.y[:, 0:w], T[b][:, o:o + w]).then_inc(S.stored, 16)
    if core in FWD:
        g.wait_ge(S.fsent, 8)
    if w > 0:
        g.wait_ge(S.stored, 16)
